import numpy as np
import ml_dtypes


def mxq(x, axis, fmt="e4m3"):
    dtype, down = {"e4m3": (ml_dtypes.float8_e4m3fn, 7), "e5m2": (ml_dtypes.float8_e5m2, 14)}[fmt]
    v = np.moveaxis(np.asarray(x, np.float32).astype(ml_dtypes.bfloat16).astype(np.float64), axis, -1)
    blocks = v.reshape(v.shape[:-1] + (-1, 32))
    amax = np.abs(blocks).max(-1, keepdims=True)
    byte = np.maximum(np.where(amax > 0, np.frexp(amax)[1] - 1 + 127, 0) - down, 1)
    scale = np.exp2(byte - 127.0)
    codes = (blocks / scale).astype(np.float32).astype(dtype).astype(np.float64)
    return np.moveaxis((codes * scale).reshape(v.shape), -1, axis)


WIDE = False


def mx_kscale(k):
    if not WIDE:
        return np.ones(k)
    levels = np.array([10, -10, 5, -5, 0])
    if k % 512:
        return np.exp2(np.random.permutation(np.resize(levels, k // 32))).repeat(32)
    a = np.empty((k // 512, 16))
    for p in range(k // 512):
        a[p, :8] = np.random.permutation(np.resize(levels, 8))
        for g in range(8):
            far = levels[np.abs(levels - a[p, g]) >= 10]
            a[p, g + 8] = far[np.random.randint(len(far))]
    return np.exp2(a.ravel()).repeat(32)


def f64(x):
    return np.asarray(x).astype(np.float64)


def striped(idx):
    return np.tile(np.asarray(idx).reshape(-1, 16).T, (8, 1)).astype(np.uint16)


def unstriped(offs):
    return offs[:16].T.reshape(-1).astype(np.int64)


E2M1 = np.array([0.0, 0.5, 1.0, 1.5, 2.0, 3.0, 4.0, 6.0, -0.0, -0.5, -1.0, -1.5, -2.0, -3.0, -4.0, -6.0])


def pack_weight(w, fmt):
    k, n = w.shape
    w = f64(np.asarray(w, np.float32).astype(ml_dtypes.bfloat16)).reshape(k // 32, 32, n)
    amax = np.abs(w).max(1)
    if fmt == "e4m3":
        byte = np.frexp(amax)[1] - 1 + 127 - 7
    else:
        mant, ex = np.frexp(amax / 6.0)
        byte = np.where(mant > 0.5, ex, ex - 1) + 127
    byte = np.clip(np.where(amax > 0, byte, 1), 1, 254)
    scaled = (w * np.exp2(127.0 - byte)[:, None, :]).reshape(k, n).astype(np.float32)
    by_word = np.ascontiguousarray(scaled.reshape(k // 512, 128, 4, n).transpose(0, 1, 3, 2))
    if fmt == "e4m3":
        words = by_word.astype(ml_dtypes.float8_e4m3fn).view(np.uint8)
    else:
        c = by_word.astype(ml_dtypes.float4_e2m1fn).view(np.uint8) & 0xF
        words = (c[..., 0::2] | (c[..., 1::2] << 4)).reshape(k // 512, 128, 2 * n)
    return np.ascontiguousarray(words), np.ascontiguousarray(byte.astype(np.uint8).reshape(k // 512, 16, n))


def unpack_weight(words, scales, fmt):
    g, _, n = scales.shape
    words = np.ascontiguousarray(words).reshape(g, 128, n, -1)
    if fmt == "e4m3":
        vals = words.view(ml_dtypes.float8_e4m3fn).astype(np.float64)
    else:
        nib = np.empty((g, 128, n, 4), np.uint8)
        nib[..., 0::2] = words & 0xF
        nib[..., 1::2] = words >> 4
        vals = E2M1[nib]
    vals = vals * np.repeat(np.exp2(scales.astype(np.float64) - 127.0), 8, axis=1)[..., None]
    return vals.transpose(0, 1, 3, 2).reshape(g * 512, n)


def bf(x):
    return np.asarray(x, np.float32).astype(ml_dtypes.bfloat16)


def planes(Y):
    r, m = Y.shape
    b = f64(bf(Y)).reshape(r // 32, 32, m)
    amax = np.abs(b).max(1)
    byte = np.clip(np.where(amax > 0, np.frexp(amax)[1] - 1 + 127 - 7, 1), 1, 254)
    codes = (b * np.exp2(127.0 - byte)[:, None, :]).reshape(r, m).astype(np.float32).astype(ml_dtypes.float8_e4m3fn).view(np.uint8)
    words = codes.reshape(r // 512, 128, 4, m).transpose(0, 1, 3, 2)
    return np.ascontiguousarray(words), np.ascontiguousarray(byte.astype(np.uint8).reshape(r // 512, 16, m))


D, T, I, J, U, X, Z, E = 512, 2048, 512, 512, 1024, 1024, 1024, 512


def setup_inputs():
    n = np.random.standard_normal
    idx = np.random.permutation(T)[:I]
    idx2 = np.random.permutation(U)[:J]
    idx3 = np.random.permutation(X)[:I]
    idx4 = np.random.permutation(Z)[:J]
    fd = mx_kscale(D)
    fi = mx_kscale(I)
    ti = np.ones(T)
    ti[idx] = fi
    keysp = pack_weight(n((D, T)) / fd[:, None], "e2m1")
    morep = pack_weight(n((D, X)) / fd[:, None], "e2m1")
    return {
        "keys_words": keysp[0],
        "keys_scales": keysp[1],
        "notes": (n((D, U)) * 1.0 / np.sqrt(D) * fd[:, None]).astype(np.float32),
        "more_words": morep[0],
        "more_scales": morep[1],
        "users2": (n((D, Z)) * 1.0 / np.sqrt(D) * fd[:, None]).astype(np.float32),
        "rowf": (np.random.uniform(0.02, 0.08, (I, 1)) * fi[:, None]).astype(np.float32),
        "vals": (n((E, T)) / ti).astype(np.float32),
        "offs": striped(idx),
        "offs2": striped(idx2),
        "offs3": striped(idx3),
        "offs4": striped(idx4),
    }


def reference(keys_words, keys_scales, notes, more_words, more_scales, users2, rowf, vals, offs, offs2, offs3, offs4):
    idx = unstriped(offs)
    idx2 = unstriped(offs2)
    idx3 = unstriped(offs3)
    idx4 = unstriped(offs4)
    keysu = unpack_weight(keys_words, keys_scales, "e2m1")
    moreu = unpack_weight(more_words, more_scales, "e2m1")
    keysidxg = keysu[:, idx]
    notesidx2q = mxq(f64(notes)[:, idx2], 0, "e4m3")
    moreidx3g = moreu[:, idx3]
    users2idx4q = mxq(f64(users2)[:, idx4], 0, "e4m3")
    g9 = keysidxg.T @ notesidx2q + moreidx3g.T @ users2idx4q
    g0 = np.maximum(g9, 0.0)
    gr1 = g0 * f64(rowf)
    vt1 = f64(vals)[:, idx].T
    vt1q = mxq(vt1, 0, "e4m3")
    gr1q = mxq(gr1, 0, "e4m3")
    o = vt1q.T @ gr1q
    words, scales = planes(o)
    return o, words, scales

@@ -1,0 +1,258 @@
+from contextlib import ExitStack
+
+import concourse.mybir as mybir
+from concourse.masks import make_identity
+
+D, T, I, J, U, X, Z, E = 512, 2048, 512, 512, 1024, 1024, 1024, 512
+FLOPS = 2 * (2 * D * I * J + I * E * J)
+
+F32 = mybir.dt.float32
+BF16 = mybir.dt.bfloat16
+I32 = mybir.dt.int32
+U32 = mybir.dt.uint32
+U16 = mybir.dt.uint16
+U8 = mybir.dt.uint8
+FP8X4 = mybir.dt.float8_e4m3fn_x4
+FP4X4 = mybir.dt.float4_e2m1fn_x4
+COPY = mybir.ActivationFunctionType.Copy
+MAX = mybir.AluOpType.max
+MULT = mybir.AluOpType.mult
+
+P = 128
+PACK = 4
+QJ = J // PACK
+HJ = J // 2
+SPLIT = 320
+
+
+def tile_attend_tab_twosum_exchange_pl_kernel(
+    tc, keys_words, keys_scales, notes, more_words, more_scales, users2, rowf, vals,
+    offs, offs2, offs3, offs4, out_0, out_1, out_2,
+):
+    nc = tc.nc
+    with ExitStack() as ctx:
+        lists = ctx.enter_context(tc.tile_pool(name="lists", bufs=1))
+        sb = ctx.enter_context(tc.tile_pool(name="sb", bufs=1))
+        ps = ctx.enter_context(tc.psum_pool(name="ps", bufs=1))
+
+        def sbuf(name, shape, dtype, tag=""):
+            return sb.tile(shape, dtype, name=name, tag=tag or name, align_bytes=64)
+
+        list_keys = lists.tile([P, I // 16], U16, name="list_keys")
+        list_notes = lists.tile([P, J // 16], U16, name="list_notes")
+        list_more = lists.tile([P, I // 16], U16, name="list_more")
+        list_users = lists.tile([P, J // 16], U16, name="list_users")
+
+        notes_pl = [sbuf("notes_pl%d" % t, [P, U], F32) for t in range(PACK)]
+        users_pl = [sbuf("users_pl%d" % t, [P, Z], F32) for t in range(PACK)]
+        vals_pl = [sbuf("vals_pl%d" % t, [P, T], F32) for t in range(PACK)]
+        keys_w = sbuf("keys_w", [P, T], U16)
+        more_w = sbuf("more_w", [P, X], U16)
+        keys_s = sbuf("keys_s", [P, T], U8)
+        more_s = sbuf("more_s", [P, X], U8)
+        rowf_t = sbuf("rowf_t", [P, PACK], F32)
+        ident = sbuf("ident", [P, P], F32)
+
+        notes_v = notes.rearrange("(p t) u -> t p u", t=PACK)
+        users_v = users2.rearrange("(p t) u -> t p u", t=PACK)
+        vals_v = vals.rearrange("(p t) u -> t p u", t=PACK)
+
+        def load_scales(dst, src, rows):
+            for r in rows:
+                nc.sync.dma_start(out=dst[:].bitcast(I32)[r:P:32, :], in_=src[0].bitcast(I32)[r:16:4, :])
+
+        nc.vector.memset(keys_s[:].bitcast(I32), 0)
+        nc.vector.memset(more_s[:].bitcast(I32), 0)
+
+        nc.sync.dma_start(out=notes_pl[0][:], in_=notes_v[0])
+        nc.sync.dma_start(list_notes[:], offs2)
+        load_scales(keys_s, keys_scales, range(4))
+        nc.sync.dma_start(list_keys[:], offs)
+        nc.sync.dma_start(out=keys_w[:].bitcast(I32), in_=keys_words[0].bitcast(I32))
+        nc.sync.dma_start(out=notes_pl[1][:], in_=notes_v[1])
+        make_identity(nc, ident[:])
+        nc.sync.dma_start(list_more[:], offs3)
+        load_scales(more_s, more_scales, range(0, 2))
+        nc.sync.dma_start(out=notes_pl[2][:], in_=notes_v[2])
+        load_scales(more_s, more_scales, range(2, 4))
+        nc.sync.dma_start(out=more_w[:].bitcast(I32), in_=more_words[0].bitcast(I32))
+        nc.sync.dma_start(out=notes_pl[3][:], in_=notes_v[3])
+        nc.sync.dma_start(out=users_pl[0][:], in_=users_v[0])
+        nc.sync.dma_start(list_users[:], offs4)
+        nc.sync.dma_start(out=users_pl[1][:], in_=users_v[1])
+        nc.sync.dma_start(out=rowf_t[:], in_=rowf.rearrange("(p r) o -> p (r o)", r=PACK))
+        nc.sync.dma_start(out=users_pl[2][:], in_=users_v[2])
+        nc.sync.dma_start(out=users_pl[3][:], in_=users_v[3])
+        for t in range(PACK):
+            nc.sync.dma_start(out=vals_pl[t][:], in_=vals_v[t])
+
+        def gather_scalar(dst, window, offsets):
+            nc.scalar.activation(dst, window[:].indirect(offsets), COPY)
+
+        def gather_vector(dst, window, offsets):
+            nc.vector.tensor_copy(dst, window[:].indirect(offsets))
+
+        def gather_both(dst, window, offsets, split):
+            count = dst.shape[1]
+            gather_vector(dst[:, 0:split], window, offsets[:, 0 : split // 16])
+            gather_scalar(dst[:, split:count], window, offsets[:, split // 16 : count // 16])
+
+        def interleave(copy, dst, src):
+            copy(
+                out=dst.rearrange("p (c i) t -> p c t i", i=4),
+                in_=src.rearrange("p t (c i) -> p c t i", i=4),
+            )
+
+        def quantize(codes, scales, src):
+            nc.vector.quantize_mx(out=codes.bitcast(FP8X4), scales=scales, in_=src)
+
+        notes_g = sbuf("notes_g", [P, PACK, J], BF16)
+        users_g = sbuf("users_g", [P, PACK, J], BF16)
+        notes_il = sbuf("notes_il", [P, J, PACK], BF16)
+        users_il = [sbuf("users_il%d" % h, [P, HJ, PACK], BF16) for h in range(2)]
+        notes_c = sbuf("notes_c", [P, J], U32)
+        notes_sc = sbuf("notes_sc", [P, J], U8)
+        users_c = sbuf("users_c", [P, J], U32)
+        users_sc = sbuf("users_sc", [P, J], U8)
+        keys_wg = sbuf("keys_wg", [P, I], U16)
+        more_wg = sbuf("more_wg", [P, I], U16)
+        keys_sg = sbuf("keys_sg", [P, I], U8)
+        more_sg = sbuf("more_sg", [P, I], U8)
+        keys_wd = sbuf("keys_wd", [P, 2 * I], U8)
+        more_wd = sbuf("more_wd", [P, 2 * I], U8)
+        scales_d = sbuf("scales_d", [P, 2 * I], U8)
+
+        def deal(dst, src):
+            nc.vector.tensor_copy(
+                out=dst.rearrange("p (r s) -> p r s", r=PACK),
+                in_=src.rearrange("p (s r) -> p r s", r=PACK),
+            )
+
+        gather_scalar(notes_g[:, 0, :], notes_pl[0], list_notes[:])
+        gather_scalar(notes_g[:, 1, :], notes_pl[1], list_notes[:])
+        gather_vector(keys_sg[:], keys_s, list_keys[:])
+        gather_vector(keys_wg[:], keys_w, list_keys[:])
+        deal(scales_d[:, 0:I], keys_sg[:])
+        gather_vector(more_sg[:], more_s, list_more[:])
+        deal(scales_d[:, I : 2 * I], more_sg[:])
+        gather_scalar(notes_g[:, 2, :], notes_pl[2], list_notes[:])
+        gather_scalar(notes_g[:, 3, :], notes_pl[3], list_notes[:])
+        deal(keys_wd[:].bitcast(U16), keys_wg[:])
+        gather_vector(more_wg[:], more_w, list_more[:])
+        deal(more_wd[:].bitcast(U16), more_wg[:])
+        interleave(nc.vector.tensor_copy, notes_il[:], notes_g[:])
+        quantize(notes_c[:], notes_sc[:], notes_il[:].rearrange("p j t -> p (j t)"))
+        gather_scalar(users_g[:, 0, :], users_pl[0], list_users[:])
+        gather_scalar(users_g[:, 1, :], users_pl[1], list_users[:])
+        gather_vector(users_g[:, 2, :], users_pl[2], list_users[:])
+        gather_both(users_g[:, 3, :], users_pl[3], list_users, HJ)
+        interleave(nc.vector.tensor_copy, users_il[0][:], users_g[:, :, 0:HJ])
+        interleave(nc.scalar.copy, users_il[1][:], users_g[:, :, HJ:J])
+        for h in range(2):
+            cols = slice(h * HJ, (h + 1) * HJ)
+            quantize(users_c[:, cols], users_sc[:, cols], users_il[h][:].rearrange("p j t -> p (j t)"))
+
+        banks = [ps.tile([P, PACK, QJ], F32, name="table%d" % q, tag="bank%d" % q) for q in range(PACK)]
+
+        def table_pass(q, r, words, first_scale, codes, scales, start, stop):
+            cols = slice(q * QJ, (q + 1) * QJ)
+            nc.tensor.matmul_mx(
+                out=banks[q][:, r, :],
+                lhsT=words[:, 2 * P * r : 2 * P * (r + 1)].bitcast(FP4X4),
+                lhsT_scale=scales_d[:, first_scale + P * r : first_scale + P * (r + 1)],
+                rhs=codes[:, cols].bitcast(FP8X4),
+                rhs_scale=scales[:, cols],
+                start=start,
+                stop=stop,
+            )
+
+        for q in range(PACK):
+            for r in range(PACK):
+                table_pass(q, r, keys_wd, 0, notes_c, notes_sc, r == 0, False)
+        for q in range(PACK):
+            for r in range(PACK):
+                table_pass(q, r, more_wd, I, users_c, users_sc, False, r == PACK - 1)
+
+        table_il = sbuf("table_il", [P, J, PACK], BF16)
+        table_c = sbuf("table_c", [P, J], U32)
+        table_sc = sbuf("table_sc", [P, J], U8)
+        for q in range(PACK):
+            nc.vector.scalar_tensor_tensor(
+                out=table_il[:, q * QJ : (q + 1) * QJ, :],
+                in0=banks[q][:].rearrange("p r j -> p j r"),
+                scalar=0.0,
+                in1=rowf_t[:].unsqueeze(1).to_broadcast([P, QJ, PACK]),
+                op0=MAX,
+                op1=MULT,
+            )
+        for h in range(2):
+            cols = slice(h * HJ, (h + 1) * HJ)
+            quantize(table_c[:, cols], table_sc[:, cols], table_il[:, cols, :].rearrange("p j r -> p (j r)"))
+
+        vals_c = [sbuf("vals_c%d" % t, [P, P], U32) for t in range(PACK)]
+        vals_sc = [sbuf("vals_sc%d" % t, [P, P], U8) for t in range(PACK)]
+
+        def values_operand(t):
+            picked = sbuf("vals_g%d" % t, [P, I], BF16)
+            if t < 2:
+                gather_scalar(picked[:], vals_pl[t], list_keys[:])
+            else:
+                gather_both(picked[:], vals_pl[t], list_keys, SPLIT)
+            pairs = picked[:].bitcast(F32)
+            turned = ps.tile([P, 2, P], F32, name="turned%d" % t, tag="turned", bufs=2)
+            for u in range(2):
+                nc.tensor.transpose(turned[:, u, :], pairs[:, u : I // 2 : 2], ident[:])
+            grouped = sbuf("vals_il%d" % t, [P, P * PACK], BF16)
+            nc.scalar.copy(
+                out=grouped[:].bitcast(F32).rearrange("p (e u) -> p e u", u=2),
+                in_=turned[:].rearrange("p u e -> p e u"),
+            )
+            quantize(vals_c[t][:], vals_sc[t][:], grouped[:])
+
+        def result_pass(t, first, last, tag):
+            bank = ps.tile([P, last - first], F32, name="result%d_%d" % (t, first), tag=tag)
+            nc.tensor.matmul_mx(
+                out=bank[:],
+                lhsT=vals_c[t][:].bitcast(FP8X4),
+                lhsT_scale=vals_sc[t][:],
+                rhs=table_c[:, first:last].bitcast(FP8X4),
+                rhs_scale=table_sc[:, first:last],
+                start=True,
+                stop=True,
+            )
+            return bank
+
+        out_v = out_0.rearrange("(p t) j -> p t j", t=PACK)
+        result = []
+        for t in range(PACK - 1):
+            values_operand(t)
+            result.append(result_pass(t, 0, J, "bank%d" % t))
+        values_operand(PACK - 1)
+        rows = sbuf("rows", [P, PACK, J], F32, "vals_pl3")
+        nc.vector.tensor_copy(out=rows[:, 0, :], in_=result[0][:])
+        nc.scalar.copy(out=rows[:, 2, :], in_=result[2][:])
+        nc.vector.tensor_copy(out=rows[:, 1, :], in_=result[1][:])
+        nc.sync.dma_start(out=out_v[:, 0 : PACK - 1, :], in_=rows[:, 0 : PACK - 1, :])
+        last = [result_pass(PACK - 1, h * HJ, (h + 1) * HJ, "bank%d" % (3 + h)) for h in range(2)]
+        for h in range(2):
+            nc.scalar.copy(out=rows[:, PACK - 1, h * HJ : (h + 1) * HJ], in_=last[h][:])
+        nc.sync.dma_start(out=out_v[:, PACK - 1, :], in_=rows[:, PACK - 1, :])
+
+        out_il = [sbuf("out_il%d" % h, [P, HJ, PACK], BF16) for h in range(2)]
+        out_c = sbuf("out_c", [P, J], U32)
+        out_sc = sbuf("out_sc", [P, J], U8)
+        words_v = out_1[0].rearrange("p c r -> p (c r)").bitcast(I32)
+        interleave(nc.vector.tensor_copy, out_il[0][:], rows[:, :, 0:HJ])
+        interleave(nc.vector.tensor_copy, out_il[1][:, 0:QJ, :], rows[:, :, HJ : HJ + QJ])
+        interleave(nc.scalar.copy, out_il[1][:, QJ:HJ, :], rows[:, :, HJ + QJ : J])
+        for h in range(2):
+            cols = slice(h * HJ, (h + 1) * HJ)
+            quantize(out_c[:, cols], out_sc[:, cols], out_il[h][:].rearrange("p j t -> p (j t)"))
+            nc.sync.dma_start(out=words_v[:, cols], in_=out_c[:, cols].bitcast(I32))
+        scale_rows = out_2[0].bitcast(I32)
+        for quad in range(4):
+            queue = nc.sync if quad % 2 == 0 else nc.scalar
+            queue.dma_start(
+                out=scale_rows[4 * quad : 4 * quad + 4, :],
+                in_=out_sc[:].bitcast(I32)[32 * quad : 32 * quad + 4, :],
+            )

@@ -33,6 +33,7 @@ def tile_attend_tab_twosum_exchange_pl_kernel(
     with ExitStack() as ctx:
         lists = ctx.enter_context(tc.tile_pool(name="lists", bufs=1))
         sb = ctx.enter_context(tc.tile_pool(name="sb", bufs=1))
+        tail = ctx.enter_context(tc.tile_pool(name="tail", bufs=1))
         ps = ctx.enter_context(tc.psum_pool(name="ps", bufs=1))
 
         def sbuf(name, shape, dtype, tag=""):
@@ -45,7 +46,8 @@ def tile_attend_tab_twosum_exchange_pl_kernel(
 
         notes_pl = [sbuf("notes_pl%d" % t, [P, U], F32) for t in range(PACK)]
         users_pl = [sbuf("users_pl%d" % t, [P, Z], F32) for t in range(PACK)]
-        vals_pl = [sbuf("vals_pl%d" % t, [P, T], F32) for t in range(PACK)]
+        vals_pl = [sbuf("vals_pl%d" % t, [P, T], F32) for t in range(PACK - 1)]
+        vals_pl.append(tail.tile([P, T], F32, name="vals_pl3", align_bytes=64, offset=0))
         keys_w = sbuf("keys_w", [P, T], U16)
         more_w = sbuf("more_w", [P, X], U16)
         keys_s = sbuf("keys_s", [P, T], U8)
@@ -192,18 +194,25 @@ def tile_attend_tab_twosum_exchange_pl_kernel(
         vals_c = [sbuf("vals_c%d" % t, [P, P], U32) for t in range(PACK)]
         vals_sc = [sbuf("vals_sc%d" % t, [P, P], U8) for t in range(PACK)]
 
-        def values_operand(t):
-            picked = sbuf("vals_g%d" % t, [P, I], BF16)
-            if t < 2:
-                gather_scalar(picked[:], vals_pl[t], list_keys[:])
+        picked = [sbuf("vals_g%d" % t, [P, I], BF16) for t in range(PACK)]
+
+        def gather_values(t):
+            if t < PACK - 1:
+                gather_scalar(picked[t][:], vals_pl[t], list_keys[:])
             else:
-                gather_both(picked[:], vals_pl[t], list_keys, SPLIT)
-            pairs = picked[:].bitcast(F32)
+                gather_both(picked[t][:], vals_pl[t], list_keys, SPLIT)
+
+        def values_operand(t):
+            pairs = picked[t][:].bitcast(F32)
             turned = ps.tile([P, 2, P], F32, name="turned%d" % t, tag="turned", bufs=2)
             for u in range(2):
                 nc.tensor.transpose(turned[:, u, :], pairs[:, u : I // 2 : 2], ident[:])
-            grouped = sbuf("vals_il%d" % t, [P, P * PACK], BF16)
-            nc.scalar.copy(
+            if t == 2:
+                grouped = tail.tile([P, P * PACK], BF16, name="vals_il2", align_bytes=64, offset=0)
+            else:
+                grouped = sbuf("vals_il%d" % t, [P, P * PACK], BF16, "vals_pl1" if t == 0 else "")
+            copy = nc.vector.tensor_copy if t == 1 else nc.scalar.copy
+            copy(
                 out=grouped[:].bitcast(F32).rearrange("p (e u) -> p e u", u=2),
                 in_=turned[:].rearrange("p u e -> p e u"),
             )
@@ -224,27 +233,32 @@ def tile_attend_tab_twosum_exchange_pl_kernel(
 
         out_v = out_0.rearrange("(p t) j -> p t j", t=PACK)
         result = []
+        gather_values(0)
         for t in range(PACK - 1):
+            gather_values(t + 1)
             values_operand(t)
             result.append(result_pass(t, 0, J, "bank%d" % t))
         values_operand(PACK - 1)
-        rows = sbuf("rows", [P, PACK, J], F32, "vals_pl3")
+        rows = tail.tile([P, PACK, J], F32, name="rows", align_bytes=64, offset=1024)
         nc.vector.tensor_copy(out=rows[:, 0, :], in_=result[0][:])
-        nc.scalar.copy(out=rows[:, 2, :], in_=result[2][:])
-        nc.vector.tensor_copy(out=rows[:, 1, :], in_=result[1][:])
-        nc.sync.dma_start(out=out_v[:, 0 : PACK - 1, :], in_=rows[:, 0 : PACK - 1, :])
-        last = [result_pass(PACK - 1, h * HJ, (h + 1) * HJ, "bank%d" % (3 + h)) for h in range(2)]
-        for h in range(2):
-            nc.scalar.copy(out=rows[:, PACK - 1, h * HJ : (h + 1) * HJ], in_=last[h][:])
+        nc.scalar.copy(out=rows[:, 1, HJ:J], in_=result[1][:, HJ:J])
+        nc.vector.tensor_copy(out=rows[:, 1, 0:HJ], in_=result[1][:, 0:HJ])
+        nc.sync.dma_start(out=out_v[:, 0:2, :], in_=rows[:, 0:2, :])
+        nc.vector.tensor_copy(out=rows[:, 2, :], in_=result[2][:])
+        nc.sync.dma_start(out=out_v[:, 2, :], in_=rows[:, 2, :])
+        last = [result_pass(PACK - 1, q * QJ, (q + 1) * QJ, "bank%d" % ((3 + q) % 6)) for q in range(PACK)]
+        for q in range(PACK):
+            nc.scalar.copy(out=rows[:, PACK - 1, q * QJ : (q + 1) * QJ], in_=last[q][:])
         nc.sync.dma_start(out=out_v[:, PACK - 1, :], in_=rows[:, PACK - 1, :])
 
         out_il = [sbuf("out_il%d" % h, [P, HJ, PACK], BF16) for h in range(2)]
         out_c = sbuf("out_c", [P, J], U32)
         out_sc = sbuf("out_sc", [P, J], U8)
         words_v = out_1[0].rearrange("p c r -> p (c r)").bitcast(I32)
-        interleave(nc.vector.tensor_copy, out_il[0][:], rows[:, :, 0:HJ])
-        interleave(nc.vector.tensor_copy, out_il[1][:, 0:QJ, :], rows[:, :, HJ : HJ + QJ])
-        interleave(nc.scalar.copy, out_il[1][:, QJ:HJ, :], rows[:, :, HJ + QJ : J])
+        for q in range(PACK):
+            copy = nc.vector.tensor_copy if q < PACK - 1 else nc.scalar.copy
+            first = (q % 2) * QJ
+            interleave(copy, out_il[q // 2][:, first : first + QJ, :], rows[:, :, q * QJ : (q + 1) * QJ])
         for h in range(2):
             cols = slice(h * HJ, (h + 1) * HJ)
             quantize(out_c[:, cols], out_sc[:, cols], out_il[h][:].rearrange("p j t -> p (j t)"))

@@ -33,6 +33,7 @@ def tile_attend_tab_twosum_exchange_pl_kernel(
     with ExitStack() as ctx:
         lists = ctx.enter_context(tc.tile_pool(name="lists", bufs=1))
         sb = ctx.enter_context(tc.tile_pool(name="sb", bufs=1))
+        third = ctx.enter_context(tc.tile_pool(name="third", bufs=1))
         tail = ctx.enter_context(tc.tile_pool(name="tail", bufs=1))
         ps = ctx.enter_context(tc.psum_pool(name="ps", bufs=1))
 
@@ -46,7 +47,8 @@ def tile_attend_tab_twosum_exchange_pl_kernel(
 
         notes_pl = [sbuf("notes_pl%d" % t, [P, U], F32) for t in range(PACK)]
         users_pl = [sbuf("users_pl%d" % t, [P, Z], F32) for t in range(PACK)]
-        vals_pl = [sbuf("vals_pl%d" % t, [P, T], F32) for t in range(PACK - 1)]
+        vals_pl = [sbuf("vals_pl%d" % t, [P, T], F32) for t in range(PACK - 2)]
+        vals_pl.append(third.tile([P, T], F32, name="vals_pl2", align_bytes=64, offset=0))
         vals_pl.append(tail.tile([P, T], F32, name="vals_pl3", align_bytes=64, offset=0))
         keys_w = sbuf("keys_w", [P, T], U16)
         more_w = sbuf("more_w", [P, X], U16)
@@ -59,34 +61,26 @@ def tile_attend_tab_twosum_exchange_pl_kernel(
         users_v = users2.rearrange("(p t) u -> t p u", t=PACK)
         vals_v = vals.rearrange("(p t) u -> t p u", t=PACK)
 
-        def load_scales(dst, src, rows):
-            for r in rows:
-                nc.sync.dma_start(out=dst[:].bitcast(I32)[r:P:32, :], in_=src[0].bitcast(I32)[r:16:4, :])
+        def load_scales(dst, src):
+            nc.sync.dma_start(out=dst[:].bitcast(I32)[0:P:8, :], in_=src[0].bitcast(I32))
 
         nc.vector.memset(keys_s[:].bitcast(I32), 0)
         nc.vector.memset(more_s[:].bitcast(I32), 0)
 
         nc.sync.dma_start(out=notes_pl[0][:], in_=notes_v[0])
         nc.sync.dma_start(list_notes[:], offs2)
-        load_scales(keys_s, keys_scales, range(4))
+        load_scales(keys_s, keys_scales)
         nc.sync.dma_start(list_keys[:], offs)
+        load_scales(more_s, more_scales)
+        nc.sync.dma_start(list_more[:], offs3)
         nc.sync.dma_start(out=keys_w[:].bitcast(I32), in_=keys_words[0].bitcast(I32))
         nc.sync.dma_start(out=notes_pl[1][:], in_=notes_v[1])
         make_identity(nc, ident[:])
-        nc.sync.dma_start(list_more[:], offs3)
-        load_scales(more_s, more_scales, range(0, 2))
         nc.sync.dma_start(out=notes_pl[2][:], in_=notes_v[2])
-        load_scales(more_s, more_scales, range(2, 4))
         nc.sync.dma_start(out=more_w[:].bitcast(I32), in_=more_words[0].bitcast(I32))
         nc.sync.dma_start(out=notes_pl[3][:], in_=notes_v[3])
-        nc.sync.dma_start(out=users_pl[0][:], in_=users_v[0])
         nc.sync.dma_start(list_users[:], offs4)
-        nc.sync.dma_start(out=users_pl[1][:], in_=users_v[1])
-        nc.sync.dma_start(out=rowf_t[:], in_=rowf.rearrange("(p r) o -> p (r o)", r=PACK))
-        nc.sync.dma_start(out=users_pl[2][:], in_=users_v[2])
-        nc.sync.dma_start(out=users_pl[3][:], in_=users_v[3])
-        for t in range(PACK):
-            nc.sync.dma_start(out=vals_pl[t][:], in_=vals_v[t])
+        nc.sync.dma_start(out=users_pl[0][:], in_=users_v[0])
 
         def gather_scalar(dst, window, offsets):
             nc.scalar.activation(dst, window[:].indirect(offsets), COPY)
@@ -123,6 +117,8 @@ def tile_attend_tab_twosum_exchange_pl_kernel(
         keys_wd = sbuf("keys_wd", [P, 2 * I], U8)
         more_wd = sbuf("more_wd", [P, 2 * I], U8)
         scales_d = sbuf("scales_d", [P, 2 * I], U8)
+        scales_mm = sbuf("scales_mm", [P, 2 * I], U8)
+        nc.vector.memset(scales_mm[:].bitcast(I32), 0)
 
         def deal(dst, src):
             nc.vector.tensor_copy(
@@ -133,10 +129,24 @@ def tile_attend_tab_twosum_exchange_pl_kernel(
         gather_scalar(notes_g[:, 0, :], notes_pl[0], list_notes[:])
         gather_scalar(notes_g[:, 1, :], notes_pl[1], list_notes[:])
         gather_vector(keys_sg[:], keys_s, list_keys[:])
-        gather_vector(keys_wg[:], keys_w, list_keys[:])
-        deal(scales_d[:, 0:I], keys_sg[:])
         gather_vector(more_sg[:], more_s, list_more[:])
+        deal(scales_d[:, 0:I], keys_sg[:])
         deal(scales_d[:, I : 2 * I], more_sg[:])
+
+        def place_scales(r):
+            nc.sync.dma_start(out=scales_mm[:].bitcast(I32)[r:P:32, :], in_=scales_d[:].bitcast(I32)[8 * r : P : 32, :])
+
+        place_scales(0)
+        place_scales(1)
+        nc.sync.dma_start(out=users_pl[1][:], in_=users_v[1])
+        place_scales(2)
+        place_scales(3)
+        nc.sync.dma_start(out=users_pl[2][:], in_=users_v[2])
+        nc.sync.dma_start(out=users_pl[3][:], in_=users_v[3])
+        nc.sync.dma_start(out=rowf_t[:], in_=rowf.rearrange("(p r) o -> p (r o)", r=PACK))
+        for t in range(PACK):
+            nc.sync.dma_start(out=vals_pl[t][:], in_=vals_v[t])
+        gather_vector(keys_wg[:], keys_w, list_keys[:])
         gather_scalar(notes_g[:, 2, :], notes_pl[2], list_notes[:])
         gather_scalar(notes_g[:, 3, :], notes_pl[3], list_notes[:])
         deal(keys_wd[:].bitcast(U16), keys_wg[:])
@@ -161,7 +171,7 @@ def tile_attend_tab_twosum_exchange_pl_kernel(
             nc.tensor.matmul_mx(
                 out=banks[q][:, r, :],
                 lhsT=words[:, 2 * P * r : 2 * P * (r + 1)].bitcast(FP4X4),
-                lhsT_scale=scales_d[:, first_scale + P * r : first_scale + P * (r + 1)],
+                lhsT_scale=scales_mm[:, first_scale + P * r : first_scale + P * (r + 1)],
                 rhs=codes[:, cols].bitcast(FP8X4),
                 rhs_scale=scales[:, cols],
                 start=start,
@@ -191,26 +201,31 @@ def tile_attend_tab_twosum_exchange_pl_kernel(
             cols = slice(h * HJ, (h + 1) * HJ)
             quantize(table_c[:, cols], table_sc[:, cols], table_il[:, cols, :].rearrange("p j r -> p (j r)"))
 
-        vals_c = [sbuf("vals_c%d" % t, [P, P], U32) for t in range(PACK)]
+        vals_c = [
+            tail.tile([P, P], U32, name="vals_c2", align_bytes=64, offset=0)
+            if t == 2
+            else sbuf("vals_c%d" % t, [P, P], U32)
+            for t in range(PACK)
+        ]
         vals_sc = [sbuf("vals_sc%d" % t, [P, P], U8) for t in range(PACK)]
 
         picked = [sbuf("vals_g%d" % t, [P, I], BF16) for t in range(PACK)]
 
         def gather_values(t):
-            if t < PACK - 1:
+            if t < 2:
                 gather_scalar(picked[t][:], vals_pl[t], list_keys[:])
             else:
                 gather_both(picked[t][:], vals_pl[t], list_keys, SPLIT)
 
         def values_operand(t):
             pairs = picked[t][:].bitcast(F32)
-            turned = ps.tile([P, 2, P], F32, name="turned%d" % t, tag="turned", bufs=2)
+            turned = ps.tile([P, 2, P], F32, name="turned%d" % t, tag="turned", bufs=3)
             for u in range(2):
                 nc.tensor.transpose(turned[:, u, :], pairs[:, u : I // 2 : 2], ident[:])
-            if t == 2:
-                grouped = tail.tile([P, P * PACK], BF16, name="vals_il2", align_bytes=64, offset=0)
+            if t < 2:
+                grouped = third.tile([P, P * PACK], BF16, name="vals_il%d" % t, align_bytes=64, offset=1024 * t)
             else:
-                grouped = sbuf("vals_il%d" % t, [P, P * PACK], BF16, "vals_pl1" if t == 0 else "")
+                grouped = sbuf("vals_il%d" % t, [P, P * PACK], BF16)
             copy = nc.vector.tensor_copy if t == 1 else nc.scalar.copy
             copy(
                 out=grouped[:].bitcast(F32).rearrange("p (e u) -> p e u", u=2),
@@ -233,20 +248,19 @@ def tile_attend_tab_twosum_exchange_pl_kernel(
 
         out_v = out_0.rearrange("(p t) j -> p t j", t=PACK)
         result = []
-        gather_values(0)
+        for t in range(PACK):
+            gather_values(t)
         for t in range(PACK - 1):
-            gather_values(t + 1)
             values_operand(t)
             result.append(result_pass(t, 0, J, "bank%d" % t))
         values_operand(PACK - 1)
         rows = tail.tile([P, PACK, J], F32, name="rows", align_bytes=64, offset=1024)
         nc.vector.tensor_copy(out=rows[:, 0, :], in_=result[0][:])
-        nc.scalar.copy(out=rows[:, 1, HJ:J], in_=result[1][:, HJ:J])
-        nc.vector.tensor_copy(out=rows[:, 1, 0:HJ], in_=result[1][:, 0:HJ])
+        nc.scalar.copy(out=rows[:, 1, :], in_=result[1][:])
         nc.sync.dma_start(out=out_v[:, 0:2, :], in_=rows[:, 0:2, :])
-        nc.vector.tensor_copy(out=rows[:, 2, :], in_=result[2][:])
+        nc.scalar.copy(out=rows[:, 2, :], in_=result[2][:])
         nc.sync.dma_start(out=out_v[:, 2, :], in_=rows[:, 2, :])
-        last = [result_pass(PACK - 1, q * QJ, (q + 1) * QJ, "bank%d" % ((3 + q) % 6)) for q in range(PACK)]
+        last = [result_pass(PACK - 1, q * QJ, (q + 1) * QJ, "bank%d" % ((3 + q) % 5)) for q in range(PACK)]
         for q in range(PACK):
             nc.scalar.copy(out=rows[:, PACK - 1, q * QJ : (q + 1) * QJ], in_=last[q][:])
         nc.sync.dma_start(out=out_v[:, PACK - 1, :], in_=rows[:, PACK - 1, :])

from contextlib import ExitStack

import concourse.mybir as mybir
from concourse.masks import make_identity

D, T, I, J, U, X, Z, E = 512, 2048, 512, 512, 1024, 1024, 1024, 512
FLOPS = 2 * (2 * D * I * J + I * E * J)

F32 = mybir.dt.float32
BF16 = mybir.dt.bfloat16
I32 = mybir.dt.int32
U32 = mybir.dt.uint32
U16 = mybir.dt.uint16
U8 = mybir.dt.uint8
FP8X4 = mybir.dt.float8_e4m3fn_x4
FP4X4 = mybir.dt.float4_e2m1fn_x4
COPY = mybir.ActivationFunctionType.Copy
MAX = mybir.AluOpType.max
MULT = mybir.AluOpType.mult

P = 128
PACK = 4
QJ = J // PACK
HJ = J // 2
SPLIT = 320


def tile_attend_tab_twosum_exchange_pl_kernel(
    tc, keys_words, keys_scales, notes, more_words, more_scales, users2, rowf, vals,
    offs, offs2, offs3, offs4, out_0, out_1, out_2,
):
    nc = tc.nc
    with ExitStack() as ctx:
        lists = ctx.enter_context(tc.tile_pool(name="lists", bufs=1))
        sb = ctx.enter_context(tc.tile_pool(name="sb", bufs=1))
        third = ctx.enter_context(tc.tile_pool(name="third", bufs=1))
        tail = ctx.enter_context(tc.tile_pool(name="tail", bufs=1))
        ps = ctx.enter_context(tc.psum_pool(name="ps", bufs=1))

        def sbuf(name, shape, dtype, tag=""):
            return sb.tile(shape, dtype, name=name, tag=tag or name, align_bytes=64)

        list_keys = lists.tile([P, I // 16], U16, name="list_keys")
        list_notes = lists.tile([P, J // 16], U16, name="list_notes")
        list_more = lists.tile([P, I // 16], U16, name="list_more")
        list_users = lists.tile([P, J // 16], U16, name="list_users")

        notes_pl = [sbuf("notes_pl%d" % t, [P, U], F32) for t in range(PACK)]
        users_pl = [sbuf("users_pl%d" % t, [P, Z], F32) for t in range(PACK)]
        vals_pl = [sbuf("vals_pl%d" % t, [P, T], F32) for t in range(PACK - 2)]
        vals_pl.append(third.tile([P, T], F32, name="vals_pl2", align_bytes=64, offset=0))
        vals_pl.append(tail.tile([P, T], F32, name="vals_pl3", align_bytes=64, offset=0))
        keys_w = sbuf("keys_w", [P, T], U16)
        more_w = sbuf("more_w", [P, X], U16)
        keys_s = sbuf("keys_s", [P, T], U8)
        more_s = sbuf("more_s", [P, X], U8)
        rowf_t = sbuf("rowf_t", [P, PACK], F32)
        ident = sbuf("ident", [P, P], F32)

        notes_v = notes.rearrange("(p t) u -> t p u", t=PACK)
        users_v = users2.rearrange("(p t) u -> t p u", t=PACK)
        vals_v = vals.rearrange("(p t) u -> t p u", t=PACK)

        def load_scales(dst, src):
            nc.sync.dma_start(out=dst[:].bitcast(I32)[0:P:8, :], in_=src[0].bitcast(I32))

        nc.vector.memset(keys_s[:].bitcast(I32), 0)
        nc.vector.memset(more_s[:].bitcast(I32), 0)

        nc.sync.dma_start(out=notes_pl[0][:], in_=notes_v[0])
        nc.sync.dma_start(list_notes[:], offs2)
        load_scales(keys_s, keys_scales)
        nc.sync.dma_start(list_keys[:], offs)
        load_scales(more_s, more_scales)
        nc.sync.dma_start(list_more[:], offs3)
        nc.sync.dma_start(out=keys_w[:].bitcast(I32), in_=keys_words[0].bitcast(I32))
        nc.sync.dma_start(out=notes_pl[1][:], in_=notes_v[1])
        make_identity(nc, ident[:])
        nc.sync.dma_start(out=notes_pl[2][:], in_=notes_v[2])
        nc.sync.dma_start(out=more_w[:].bitcast(I32), in_=more_words[0].bitcast(I32))
        nc.sync.dma_start(out=notes_pl[3][:], in_=notes_v[3])
        nc.sync.dma_start(list_users[:], offs4)
        nc.sync.dma_start(out=users_pl[0][:], in_=users_v[0])

        def gather_scalar(dst, window, offsets):
            nc.scalar.activation(dst, window[:].indirect(offsets), COPY)

        def gather_vector(dst, window, offsets):
            nc.vector.tensor_copy(dst, window[:].indirect(offsets))

        def gather_both(dst, window, offsets, split):
            count = dst.shape[1]
            gather_vector(dst[:, 0:split], window, offsets[:, 0 : split // 16])
            gather_scalar(dst[:, split:count], window, offsets[:, split // 16 : count // 16])

        def interleave(copy, dst, src):
            copy(
                out=dst.rearrange("p (c i) t -> p c t i", i=4),
                in_=src.rearrange("p t (c i) -> p c t i", i=4),
            )

        def quantize(codes, scales, src):
            nc.vector.quantize_mx(out=codes.bitcast(FP8X4), scales=scales, in_=src)

        notes_g = sbuf("notes_g", [P, PACK, J], BF16)
        users_g = sbuf("users_g", [P, PACK, J], BF16)
        notes_il = sbuf("notes_il", [P, J, PACK], BF16)
        users_il = [sbuf("users_il%d" % h, [P, HJ, PACK], BF16) for h in range(2)]
        notes_c = sbuf("notes_c", [P, J], U32)
        notes_sc = sbuf("notes_sc", [P, J], U8)
        users_c = sbuf("users_c", [P, J], U32)
        users_sc = sbuf("users_sc", [P, J], U8)
        keys_wg = sbuf("keys_wg", [P, I], U16)
        more_wg = sbuf("more_wg", [P, I], U16)
        keys_sg = sbuf("keys_sg", [P, I], U8)
        more_sg = sbuf("more_sg", [P, I], U8)
        keys_wd = sbuf("keys_wd", [P, 2 * I], U8)
        more_wd = sbuf("more_wd", [P, 2 * I], U8)
        scales_d = sbuf("scales_d", [P, 2 * I], U8)
        scales_mm = sbuf("scales_mm", [P, 2 * I], U8)
        nc.vector.memset(scales_mm[:].bitcast(I32), 0)

        def deal(dst, src):
            nc.vector.tensor_copy(
                out=dst.rearrange("p (r s) -> p r s", r=PACK),
                in_=src.rearrange("p (s r) -> p r s", r=PACK),
            )

        gather_scalar(notes_g[:, 0, :], notes_pl[0], list_notes[:])
        gather_scalar(notes_g[:, 1, :], notes_pl[1], list_notes[:])
        gather_vector(keys_sg[:], keys_s, list_keys[:])
        gather_vector(more_sg[:], more_s, list_more[:])
        deal(scales_d[:, 0:I], keys_sg[:])
        deal(scales_d[:, I : 2 * I], more_sg[:])

        def place_scales(r):
            nc.sync.dma_start(out=scales_mm[:].bitcast(I32)[r:P:32, :], in_=scales_d[:].bitcast(I32)[8 * r : P : 32, :])

        place_scales(0)
        place_scales(1)
        nc.sync.dma_start(out=users_pl[1][:], in_=users_v[1])
        place_scales(2)
        place_scales(3)
        nc.sync.dma_start(out=users_pl[2][:], in_=users_v[2])
        nc.sync.dma_start(out=users_pl[3][:], in_=users_v[3])
        nc.sync.dma_start(out=rowf_t[:], in_=rowf.rearrange("(p r) o -> p (r o)", r=PACK))
        for t in range(PACK):
            nc.sync.dma_start(out=vals_pl[t][:], in_=vals_v[t])
        gather_vector(keys_wg[:], keys_w, list_keys[:])
        gather_scalar(notes_g[:, 2, :], notes_pl[2], list_notes[:])
        gather_scalar(notes_g[:, 3, :], notes_pl[3], list_notes[:])
        deal(keys_wd[:].bitcast(U16), keys_wg[:])
        gather_vector(more_wg[:], more_w, list_more[:])
        deal(more_wd[:].bitcast(U16), more_wg[:])
        interleave(nc.vector.tensor_copy, notes_il[:], notes_g[:])
        quantize(notes_c[:], notes_sc[:], notes_il[:].rearrange("p j t -> p (j t)"))
        gather_scalar(users_g[:, 0, :], users_pl[0], list_users[:])
        gather_scalar(users_g[:, 1, :], users_pl[1], list_users[:])
        gather_vector(users_g[:, 2, :], users_pl[2], list_users[:])
        gather_both(users_g[:, 3, :], users_pl[3], list_users, HJ)
        interleave(nc.vector.tensor_copy, users_il[0][:], users_g[:, :, 0:HJ])
        interleave(nc.scalar.copy, users_il[1][:], users_g[:, :, HJ:J])
        for h in range(2):
            cols = slice(h * HJ, (h + 1) * HJ)
            quantize(users_c[:, cols], users_sc[:, cols], users_il[h][:].rearrange("p j t -> p (j t)"))

        banks = [ps.tile([P, PACK, QJ], F32, name="table%d" % q, tag="bank%d" % q) for q in range(PACK)]

        def table_pass(q, r, words, first_scale, codes, scales, start, stop):
            cols = slice(q * QJ, (q + 1) * QJ)
            nc.tensor.matmul_mx(
                out=banks[q][:, r, :],
                lhsT=words[:, 2 * P * r : 2 * P * (r + 1)].bitcast(FP4X4),
                lhsT_scale=scales_mm[:, first_scale + P * r : first_scale + P * (r + 1)],
                rhs=codes[:, cols].bitcast(FP8X4),
                rhs_scale=scales[:, cols],
                start=start,
                stop=stop,
            )

        for q in range(PACK):
            for r in range(PACK):
                table_pass(q, r, keys_wd, 0, notes_c, notes_sc, r == 0, False)
        for q in range(PACK):
            for r in range(PACK):
                table_pass(q, r, more_wd, I, users_c, users_sc, False, r == PACK - 1)

        table_il = sbuf("table_il", [P, J, PACK], BF16)
        table_c = sbuf("table_c", [P, J], U32)
        table_sc = sbuf("table_sc", [P, J], U8)
        for q in range(PACK):
            nc.vector.scalar_tensor_tensor(
                out=table_il[:, q * QJ : (q + 1) * QJ, :],
                in0=banks[q][:].rearrange("p r j -> p j r"),
                scalar=0.0,
                in1=rowf_t[:].unsqueeze(1).to_broadcast([P, QJ, PACK]),
                op0=MAX,
                op1=MULT,
            )
        for h in range(2):
            cols = slice(h * HJ, (h + 1) * HJ)
            quantize(table_c[:, cols], table_sc[:, cols], table_il[:, cols, :].rearrange("p j r -> p (j r)"))

        vals_c = [
            tail.tile([P, P], U32, name="vals_c2", align_bytes=64, offset=0)
            if t == 2
            else sbuf("vals_c%d" % t, [P, P], U32)
            for t in range(PACK)
        ]
        vals_sc = [sbuf("vals_sc%d" % t, [P, P], U8) for t in range(PACK)]

        picked = [sbuf("vals_g%d" % t, [P, I], BF16) for t in range(PACK)]

        def gather_values(t):
            if t < 2:
                gather_scalar(picked[t][:], vals_pl[t], list_keys[:])
            else:
                gather_both(picked[t][:], vals_pl[t], list_keys, SPLIT)

        def values_operand(t):
            pairs = picked[t][:].bitcast(F32)
            turned = ps.tile([P, 2, P], F32, name="turned%d" % t, tag="turned", bufs=3)
            for u in range(2):
                nc.tensor.transpose(turned[:, u, :], pairs[:, u : I // 2 : 2], ident[:])
            if t < 2:
                grouped = third.tile([P, P * PACK], BF16, name="vals_il%d" % t, align_bytes=64, offset=1024 * t)
            else:
                grouped = sbuf("vals_il%d" % t, [P, P * PACK], BF16)
            copy = nc.vector.tensor_copy if t == 1 else nc.scalar.copy
            copy(
                out=grouped[:].bitcast(F32).rearrange("p (e u) -> p e u", u=2),
                in_=turned[:].rearrange("p u e -> p e u"),
            )
            quantize(vals_c[t][:], vals_sc[t][:], grouped[:])

        def result_pass(t, first, last, tag):
            bank = ps.tile([P, last - first], F32, name="result%d_%d" % (t, first), tag=tag)
            nc.tensor.matmul_mx(
                out=bank[:],
                lhsT=vals_c[t][:].bitcast(FP8X4),
                lhsT_scale=vals_sc[t][:],
                rhs=table_c[:, first:last].bitcast(FP8X4),
                rhs_scale=table_sc[:, first:last],
                start=True,
                stop=True,
            )
            return bank

        out_v = out_0.rearrange("(p t) j -> p t j", t=PACK)
        result = []
        for t in range(PACK):
            gather_values(t)
        for t in range(PACK - 1):
            values_operand(t)
            result.append(result_pass(t, 0, J, "bank%d" % t))
        values_operand(PACK - 1)
        rows = tail.tile([P, PACK, J], F32, name="rows", align_bytes=64, offset=1024)
        nc.vector.tensor_copy(out=rows[:, 0, :], in_=result[0][:])
        nc.scalar.copy(out=rows[:, 1, :], in_=result[1][:])
        nc.sync.dma_start(out=out_v[:, 0:2, :], in_=rows[:, 0:2, :])
        nc.scalar.copy(out=rows[:, 2, :], in_=result[2][:])
        nc.sync.dma_start(out=out_v[:, 2, :], in_=rows[:, 2, :])
        last = [result_pass(PACK - 1, q * QJ, (q + 1) * QJ, "bank%d" % ((3 + q) % 5)) for q in range(PACK)]
        for q in range(PACK):
            nc.scalar.copy(out=rows[:, PACK - 1, q * QJ : (q + 1) * QJ], in_=last[q][:])
        nc.sync.dma_start(out=out_v[:, PACK - 1, :], in_=rows[:, PACK - 1, :])

        out_il = [sbuf("out_il%d" % h, [P, HJ, PACK], BF16) for h in range(2)]
        out_c = sbuf("out_c", [P, J], U32)
        out_sc = sbuf("out_sc", [P, J], U8)
        words_v = out_1[0].rearrange("p c r -> p (c r)").bitcast(I32)
        for q in range(PACK):
            copy = nc.vector.tensor_copy if q < PACK - 1 else nc.scalar.copy
            first = (q % 2) * QJ
            interleave(copy, out_il[q // 2][:, first : first + QJ, :], rows[:, :, q * QJ : (q + 1) * QJ])
        for h in range(2):
            cols = slice(h * HJ, (h + 1) * HJ)
            quantize(out_c[:, cols], out_sc[:, cols], out_il[h][:].rearrange("p j t -> p (j t)"))
            nc.sync.dma_start(out=words_v[:, cols], in_=out_c[:, cols].bitcast(I32))
        scale_rows = out_2[0].bitcast(I32)
        for quad in range(4):
            queue = nc.sync if quad % 2 == 0 else nc.scalar
            queue.dma_start(
                out=scale_rows[4 * quad : 4 * quad + 4, :],
                in_=out_sc[:].bitcast(I32)[32 * quad : 32 * quad + 4, :],
            )
